import numpy as np
import ml_dtypes


def mxq(x, axis, fmt="e4m3"):
    dtype, down = {"e4m3": (ml_dtypes.float8_e4m3fn, 7), "e5m2": (ml_dtypes.float8_e5m2, 14)}[fmt]
    v = np.moveaxis(np.asarray(x, np.float32).astype(ml_dtypes.bfloat16).astype(np.float64), axis, -1)
    blocks = v.reshape(v.shape[:-1] + (-1, 32))
    amax = np.abs(blocks).max(-1, keepdims=True)
    byte = np.maximum(np.where(amax > 0, np.frexp(amax)[1] - 1 + 127, 0) - down, 1)
    scale = np.exp2(byte - 127.0)
    codes = (blocks / scale).astype(np.float32).astype(dtype).astype(np.float64)
    return np.moveaxis((codes * scale).reshape(v.shape), -1, axis)


WIDE = False


def mx_kscale(k):
    if not WIDE:
        return np.ones(k)
    levels = np.array([10, -10, 5, -5, 0])
    if k % 512:
        return np.exp2(np.random.permutation(np.resize(levels, k // 32))).repeat(32)
    a = np.empty((k // 512, 16))
    for p in range(k // 512):
        a[p, :8] = np.random.permutation(np.resize(levels, 8))
        for g in range(8):
            far = levels[np.abs(levels - a[p, g]) >= 10]
            a[p, g + 8] = far[np.random.randint(len(far))]
    return np.exp2(a.ravel()).repeat(32)


def f64(x):
    return np.asarray(x).astype(np.float64)


def striped(idx):
    return np.tile(idx.reshape(-1, 16).T, (8, 1)).astype(np.uint16)


def unstriped(offs):
    return offs[:16].T.reshape(-1).astype(np.int64)


def relu2(v):
    return np.maximum(v, 0.0) ** 2


K, T, S, H, N = 2048, 1024, 512, 512, 512


def setup_inputs():
    n = np.random.standard_normal
    s = mx_kscale(K)[:, None]
    u = mx_kscale(H)
    return {
        "xT": (n((K, S)) * s).astype(np.float32),
        "w1": (n((K, H)) / np.sqrt(K) / s * u).astype(np.float32),
        "w2": (n((H, N)) / np.sqrt(H) / u[:, None] ** 2).astype(np.float32),
        "gate": np.tile(np.random.uniform(0.2, 1.0, S), (N, 1)).astype(np.float32),
        "offs": striped(np.random.permutation(T)[:S]),
    }


def reference(xT, w1, w2, gate, offs):
    idx = unstriped(offs)
    xq = mxq(f64(xT), 0, "e4m3")
    h = relu2(mxq(f64(w1), 0, "e4m3").T @ xq)
    y = mxq(f64(w2), 0, "e4m3").T @ mxq(h, 0, "e4m3")
    out = np.zeros((N, T))
    out[:, idx] = f64(gate) * y
    return out

@@ -1,0 +1,266 @@
+from contextlib import ExitStack
+
+import concourse.mybir as mybir
+
+K, S, H, N, T = 2048, 512, 512, 512, 1024
+FLOPS = 2 * S * (K * H + H * N)
+
+F32 = mybir.dt.float32
+BF16 = mybir.dt.bfloat16
+U32 = mybir.dt.uint32
+U16 = mybir.dt.uint16
+U8 = mybir.dt.uint8
+FP8X4 = mybir.dt.float8_e4m3fn_x4
+ACT = mybir.ActivationFunctionType
+MULT = mybir.AluOpType.mult
+ADD = mybir.AluOpType.add
+MAX = mybir.AluOpType.max
+
+P = 128
+PACK = 4
+PASSES = K // (P * PACK)
+BLOCKS = N // P
+
+CHUNKS = [[0,128],[128,128],[256,256]]
+X_CAST = ["VSSS","VSSS","SVSS"]
+W1_CAST = ["SS","VS","VS","VV"]
+W2_CAST = "VS"
+MERGE = [False,True,True]
+RELU = ["VVVV","SVVS","SSSV"]
+SQUARE = ["V","S","S"]
+Y_COPY = ["S","S","S"]
+LOADS = ["w3","w2","w0","x0","w1","x1","v","o","g0","x2","g2","g1"]
+STEPS = ["W3","W2","W1","W0","q0","q1","c00","f00","c02","c01","f01","q2","f02","q3","c03","f03","V","h0","X1","Q","y0","h1","X2","S0","y1","h2","y2","E12"]
+FUSED = True
+
+
+def tile_picked_place_mlp_relu2_sub_l_kernel(tc, xT, w1, w2, gate, offs, out):
+    nc = tc.nc
+    with ExitStack() as ctx:
+        held = ctx.enter_context(tc.tile_pool(name="held", bufs=1))
+        psum = ctx.enter_context(tc.psum_pool(name="psum", bufs=1))
+
+        def sb(shape, dtype, name):
+            return held.tile(shape, dtype, name=name, align_bytes=64)
+
+        offsets = held.tile([P, S // 16], U16, name="offsets")
+        warm = sb([P, 16], F32, "warm")
+        windows = [sb([P, T], F32, f"window{m}") for m in range(BLOCKS)]
+
+        w1_raw = [sb([P, PACK, H], F32, f"w1_raw{p}") for p in range(PASSES)]
+        x_raw = [[sb([P, PACK, n], F32, f"x_raw{c}_{p}") for p in range(PASSES)] for c, (s, n) in enumerate(CHUNKS)]
+        w2_raw = sb([P, PACK, N], F32, "w2_raw")
+        gates = [sb([P, BLOCKS, n], F32, f"gate{c}") for c, (s, n) in enumerate(CHUNKS)]
+
+        def rows(p):
+            return slice(p * P * PACK, (p + 1) * P * PACK)
+
+        def load_x(c):
+            s, n = CHUNKS[c]
+            for p in range(PASSES):
+                nc.sync.dma_start(out=x_raw[c][p][:], in_=xT[rows(p), s : s + n].rearrange("(p j) w -> p j w", j=PACK))
+
+        def load_gate(c):
+            s, n = CHUNKS[c]
+            nc.sync.dma_start(out=gates[c][:], in_=gate[:, s : s + n].rearrange("(m p) w -> p m w", p=P))
+
+        for token in LOADS:
+            kind, index = token[0], int(token[1:] or 0)
+            if kind == "w":
+                nc.sync.dma_start(out=w1_raw[index][:], in_=w1[rows(index), :].rearrange("(p j) w -> p j w", j=PACK))
+            elif kind == "x":
+                load_x(index)
+            elif kind == "v":
+                nc.sync.dma_start(out=w2_raw[:], in_=w2.rearrange("(p j) w -> p j w", j=PACK))
+            elif kind == "o":
+                nc.sync.dma_start(offsets[:], offs)
+            elif kind == "g":
+                load_gate(index)
+
+        nc.vector.memset(warm[:], 0.0)
+        nc.scalar.activation(warm[:], warm[:], ACT.Relu)
+        for m in range(BLOCKS):
+            nc.vector.memset(windows[m][:], 0.0)
+
+        def cast(engine, out, in_):
+            if engine == "V":
+                nc.vector.tensor_copy(out=out, in_=in_)
+            elif engine == "G":
+                nc.gpsimd.tensor_scalar(out, in_, 1.0, 0.0, MULT, ADD)
+            else:
+                nc.scalar.copy(out=out, in_=in_)
+
+        def quantize(codes, scales, grouped):
+            nc.vector.quantize_mx(out=codes[:].bitcast(FP8X4), scales=scales[:], in_=grouped)
+
+        HALF = H // 2
+        w1_codes = [[sb([P, HALF], U32, f"w1_codes{p}_{i}") for i in range(2)] for p in range(PASSES)]
+        w1_scales = [[sb([P, HALF], U8, f"w1_scales{p}_{i}") for i in range(2)] for p in range(PASSES)]
+
+        w1_bf = [[sb([P, HALF * PACK], BF16, f"w1_bf{p}_{i}") for i in range(2)] for p in range(PASSES)]
+
+        def cast_w1(p):
+            for i, engine in enumerate(W1_CAST[p]):
+                cast(
+                    engine,
+                    w1_bf[p][i][:].rearrange("p (t m j) -> p m t j", t=2, j=PACK),
+                    w1_raw[p][:].rearrange("p j (m t) -> p m t j", t=PACK)[:, :, 2 * i : 2 * i + 2, :],
+                )
+
+        def quant_w1(p):
+            for i in range(2):
+                quantize(w1_codes[p][i], w1_scales[p][i], w1_bf[p][i][:])
+
+        w2_bf = [sb([P, HALF * PACK], BF16, f"w2_bf{i}") for i in range(2)]
+        w2_codes = [sb([P, HALF], U32, f"w2_codes{i}") for i in range(2)]
+        w2_scales = [sb([P, HALF], U8, f"w2_scales{i}") for i in range(2)]
+
+        def cast_w2():
+            for i, engine in enumerate(W2_CAST):
+                cast(
+                    engine,
+                    w2_bf[i][:].rearrange("p (c j) -> p c j", j=PACK),
+                    w2_raw[:].rearrange("p j c -> p c j")[:, i * HALF : (i + 1) * HALF, :],
+                )
+
+        def quant_w2():
+            for i in range(2):
+                quantize(w2_codes[i], w2_scales[i], w2_bf[i][:])
+
+        x_bf = [[sb([P, n * PACK], BF16, f"x_bf{c}_{p}") for p in range(PASSES)] for c, (s, n) in enumerate(CHUNKS)]
+        x_codes = [[sb([P, n], U32, f"x_codes{c}_{p}") for p in range(PASSES)] for c, (s, n) in enumerate(CHUNKS)]
+        x_scales = [[sb([P, n], U8, f"x_scales{c}_{p}") for p in range(PASSES)] for c, (s, n) in enumerate(CHUNKS)]
+
+        def cast_x(c, p):
+            cast(
+                X_CAST[c][p],
+                x_bf[c][p][:].rearrange("p (c j) -> p c j", j=PACK),
+                x_raw[c][p][:].rearrange("p j c -> p c j"),
+            )
+
+        def quant_x(c, p):
+            quantize(x_codes[c][p], x_scales[c][p], x_bf[c][p][:])
+
+        h_ps = {}
+
+        def product(c, t, p, bank):
+            cols = slice((t % 2) * P, (t % 2 + 1) * P)
+            nc.tensor.matmul_mx(
+                out=bank,
+                lhsT=w1_codes[p][t // 2][:, cols].bitcast(FP8X4),
+                lhsT_scale=w1_scales[p][t // 2][:, cols],
+                rhs=x_codes[c][p][:].bitcast(FP8X4),
+                rhs_scale=x_scales[c][p][:],
+                start=(p == 0),
+                stop=(p == PASSES - 1),
+            )
+
+        def first(c, p):
+            n = CHUNKS[c][1]
+            if MERGE[c]:
+                return
+            for t in range(PACK):
+                if p == 0:
+                    h_ps[c, t] = psum.tile([P, n], F32, name=f"h_ps{t}", tag=f"h_ps{t}")
+                product(c, t, p, h_ps[c, t][:])
+
+        relu = [sb([P, PACK, n], F32, f"relu{c}") for c, (s, n) in enumerate(CHUNKS)]
+        h_bf = [sb([P, n * PACK], BF16, f"h_bf{c}") for c, (s, n) in enumerate(CHUNKS)]
+        h_codes = [sb([P, n], U32, f"h_codes{c}") for c, (s, n) in enumerate(CHUNKS)]
+        h_scales = [sb([P, n], U8, f"h_scales{c}") for c, (s, n) in enumerate(CHUNKS)]
+        y_sb = [sb([P, BLOCKS, n], F32, f"y_sb{c}") for c, (s, n) in enumerate(CHUNKS)]
+
+        def hidden(c):
+            n = CHUNKS[c][1]
+            if MERGE[c]:
+                per = 512 // n
+                for b in range(PACK // per):
+                    bank = psum.tile([P, per, n], F32, name=f"h_ps{b}", tag=f"h_ps{b + 2 * (c % 2)}")
+                    for i in range(per):
+                        for p in range(PASSES):
+                            product(c, b * per + i, p, bank[:, i, :])
+                    relu_to(RELU[c][b], relu[c][:, b * per : (b + 1) * per, :], bank[:])
+            else:
+                for t in range(PACK):
+                    relu_to(RELU[c][t], relu[c][:, t, :], h_ps[c, t][:])
+            src = relu[c][:].rearrange("p t n -> p n t")
+            dst = h_bf[c][:].rearrange("p (n t) -> p n t", t=PACK)
+            if SQUARE[c] == "V":
+                nc.vector.tensor_tensor(dst, src, src, MULT)
+            elif SQUARE[c] == "G":
+                nc.gpsimd.tensor_tensor(dst, src, src, MULT)
+            else:
+                nc.scalar.activation(dst, src, ACT.Square)
+            quantize(h_codes[c], h_scales[c], h_bf[c][:])
+
+        def relu_to(engine, out, in_):
+            if engine == "V":
+                nc.vector.tensor_scalar(out, in_, 0.0, None, MAX)
+            else:
+                nc.scalar.activation(out, in_, ACT.Relu)
+
+        def second(c):
+            n = CHUNKS[c][1]
+            per = 512 // n
+            for b in range(BLOCKS // per):
+                y_ps = psum.tile([P, per, n], F32, name=f"y_ps{c}_{b}", tag="y_ps", bufs=4)
+                for i in range(per):
+                    m = b * per + i
+                    cols = slice((m % 2) * P, (m % 2 + 1) * P)
+                    nc.tensor.matmul_mx(
+                        out=y_ps[:, i, :],
+                        lhsT=w2_codes[m // 2][:, cols].bitcast(FP8X4),
+                        lhsT_scale=w2_scales[m // 2][:, cols],
+                        rhs=h_codes[c][:].bitcast(FP8X4),
+                        rhs_scale=h_scales[c][:],
+                        start=True,
+                        stop=True,
+                    )
+                blocks = slice(b * per, (b + 1) * per)
+                if not FUSED:
+                    nc.vector.tensor_tensor(y_sb[c][:, blocks, :], y_ps[:], gates[c][:, blocks, :], MULT)
+                elif Y_COPY[c] == "V":
+                    nc.vector.tensor_copy(out=y_sb[c][:, blocks, :], in_=y_ps[:])
+                else:
+                    nc.scalar.copy(out=y_sb[c][:, blocks, :], in_=y_ps[:])
+
+        def scatter(c, m):
+            s, n = CHUNKS[c]
+            window = windows[m][:].indirect(offsets[:, s // 16 : (s + n) // 16])
+            if FUSED:
+                nc.vector.tensor_tensor(window, y_sb[c][:, m, :], gates[c][:, m, :], MULT)
+            else:
+                nc.vector.tensor_copy(window, y_sb[c][:, m, :])
+
+        for token in STEPS:
+            kind, index = token[0], int(token[1:] or 0)
+            if kind == "W":
+                cast_w1(index)
+            elif kind == "q":
+                quant_w1(index)
+            elif kind == "c":
+                cast_x(index // 10, index % 10)
+            elif kind == "f":
+                quant_x(index // 10, index % 10)
+                first(index // 10, index % 10)
+            elif kind == "X":
+                for p in range(PASSES):
+                    cast_x(index, p)
+                    quant_x(index, p)
+                    first(index, p)
+            elif kind == "V":
+                cast_w2()
+            elif kind == "Q":
+                quant_w2()
+            elif kind == "h":
+                hidden(index)
+            elif kind == "y":
+                second(index)
+            elif kind == "S":
+                for m in range(BLOCKS):
+                    scatter(index, m)
+            elif kind == "E":
+                for m in range(BLOCKS):
+                    for c in token[1:]:
+                        scatter(int(c), m)
+                    nc.sync.dma_start(out=out[m * P : (m + 1) * P, :], in_=windows[m][:])

@@ -22,16 +22,16 @@ PASSES = K // (P * PACK)
 BLOCKS = N // P
 
 CHUNKS = [[0,128],[128,128],[256,256]]
-X_CAST = ["VSSS","VSSS","SVSS"]
-W1_CAST = ["SS","VS","VS","VV"]
-W2_CAST = "VS"
-MERGE = [False,True,True]
-RELU = ["VVVV","SVVS","SSSV"]
+X_CAST = ["VSSV","SSSS","SSSS"]
+W1_CAST = ["VS","VV","SV","VS"]
+W2_CAST = "SV"
+MERGE = [False,True,False]
+RELU = ["SVVV","VSSV","SSSV"]
 SQUARE = ["V","S","S"]
 Y_COPY = ["S","S","S"]
-LOADS = ["w3","w2","w0","x0","w1","x1","v","o","g0","x2","g2","g1"]
-STEPS = ["W3","W2","W1","W0","q0","q1","c00","f00","c02","c01","f01","q2","f02","q3","c03","f03","V","h0","X1","Q","y0","h1","X2","S0","y1","h2","y2","E12"]
-FUSED = True
+LOADS = ["w1","w2","w0","x0","w3","o","v","g0","g1","x1","x2","g2"]
+STEPS = ["W0","W1","q1","W2","q0","W3","c00","q2","q3","c01","f00","f01","c02","f02","c03","f03","V","h0","Q","y0","X1","h1","S0","y1","X2","h2","y2","E12"]
+FUSED = False
 
 
 def tile_picked_place_mlp_relu2_sub_l_kernel(tc, xT, w1, w2, gate, offs, out):

@@ -21,17 +21,18 @@ PACK = 4
 PASSES = K // (P * PACK)
 BLOCKS = N // P
 
-CHUNKS = [[0,128],[128,128],[256,256]]
-X_CAST = ["VSSV","SSSS","SSSS"]
-W1_CAST = ["VS","VV","SV","VS"]
-W2_CAST = "SV"
-MERGE = [False,True,False]
-RELU = ["SVVV","VSSV","SSSV"]
-SQUARE = ["V","S","S"]
-Y_COPY = ["S","S","S"]
-LOADS = ["w1","w2","w0","x0","w3","o","v","g0","g1","x1","x2","g2"]
-STEPS = ["W0","W1","q1","W2","q0","W3","c00","q2","q3","c01","f00","f01","c02","f02","c03","f03","V","h0","Q","y0","X1","h1","S0","y1","X2","h2","y2","E12"]
-FUSED = False
+CHUNKS = [[0,256],[256,256]]
+X_SEGS = [["S1","V2","S1"],["V2","V1","S1"]]
+XQ = [1,2]
+W1_CAST = ["V","SV","S","SV"]
+W2_CAST = "V"
+MERGE = [True,True]
+RELU = ["SSVS","SSVS"]
+SQUARE = ["S","S"]
+Y_COPY = ["S","S"]
+LOADS = ["w2","w1","w0","w3","x0","v","x1","o","g0","g1"]
+STEPS = ["V","c0","W3","W1","Q","W0","q3","q0","W2","q2","q1","f0","h0","c1","y0","f1","h1","y1","E01"]
+ZERO = "G"
 
 
 def tile_picked_place_mlp_relu2_sub_l_kernel(tc, xT, w1, w2, gate, offs, out):
@@ -46,136 +47,135 @@ def tile_picked_place_mlp_relu2_sub_l_kernel(tc, xT, w1, w2, gate, offs, out):
         offsets = held.tile([P, S // 16], U16, name="offsets")
         warm = sb([P, 16], F32, "warm")
         windows = [sb([P, T], F32, f"window{m}") for m in range(BLOCKS)]
+        sizes = [n for s, n in CHUNKS]
 
         w1_raw = [sb([P, PACK, H], F32, f"w1_raw{p}") for p in range(PASSES)]
-        x_raw = [[sb([P, PACK, n], F32, f"x_raw{c}_{p}") for p in range(PASSES)] for c, (s, n) in enumerate(CHUNKS)]
+        x_raw = [sb([P, PASSES, PACK, n], F32, f"x_raw{c}") for c, n in enumerate(sizes)]
         w2_raw = sb([P, PACK, N], F32, "w2_raw")
-        gates = [sb([P, BLOCKS, n], F32, f"gate{c}") for c, (s, n) in enumerate(CHUNKS)]
+        gates = [sb([P, BLOCKS, n], F32, f"gate{c}") for c, n in enumerate(sizes)]
 
         def rows(p):
             return slice(p * P * PACK, (p + 1) * P * PACK)
-
-        def load_x(c):
-            s, n = CHUNKS[c]
-            for p in range(PASSES):
-                nc.sync.dma_start(out=x_raw[c][p][:], in_=xT[rows(p), s : s + n].rearrange("(p j) w -> p j w", j=PACK))
-
-        def load_gate(c):
-            s, n = CHUNKS[c]
-            nc.sync.dma_start(out=gates[c][:], in_=gate[:, s : s + n].rearrange("(m p) w -> p m w", p=P))
 
         for token in LOADS:
             kind, index = token[0], int(token[1:] or 0)
             if kind == "w":
                 nc.sync.dma_start(out=w1_raw[index][:], in_=w1[rows(index), :].rearrange("(p j) w -> p j w", j=PACK))
             elif kind == "x":
-                load_x(index)
+                s, n = CHUNKS[index]
+                for p in range(PASSES):
+                    nc.sync.dma_start(
+                        out=x_raw[index][:, p], in_=xT[rows(p), s : s + n].rearrange("(p j) w -> p j w", j=PACK)
+                    )
             elif kind == "v":
                 nc.sync.dma_start(out=w2_raw[:], in_=w2.rearrange("(p j) w -> p j w", j=PACK))
             elif kind == "o":
                 nc.sync.dma_start(offsets[:], offs)
             elif kind == "g":
-                load_gate(index)
+                s, n = CHUNKS[index]
+                nc.sync.dma_start(out=gates[index][:], in_=gate[:, s : s + n].rearrange("(m p) w -> p m w", p=P))
 
         nc.vector.memset(warm[:], 0.0)
         nc.scalar.activation(warm[:], warm[:], ACT.Relu)
         for m in range(BLOCKS):
-            nc.vector.memset(windows[m][:], 0.0)
+            if ZERO == "G":
+                nc.gpsimd.memset(windows[m][:], 0.0)
+            else:
+                nc.vector.memset(windows[m][:], 0.0)
 
         def cast(engine, out, in_):
             if engine == "V":
                 nc.vector.tensor_copy(out=out, in_=in_)
-            elif engine == "G":
-                nc.gpsimd.tensor_scalar(out, in_, 1.0, 0.0, MULT, ADD)
             else:
                 nc.scalar.copy(out=out, in_=in_)
 
         def quantize(codes, scales, grouped):
-            nc.vector.quantize_mx(out=codes[:].bitcast(FP8X4), scales=scales[:], in_=grouped)
+            nc.vector.quantize_mx(out=codes.bitcast(FP8X4), scales=scales, in_=grouped)
 
-        HALF = H // 2
-        w1_codes = [[sb([P, HALF], U32, f"w1_codes{p}_{i}") for i in range(2)] for p in range(PASSES)]
-        w1_scales = [[sb([P, HALF], U8, f"w1_scales{p}_{i}") for i in range(2)] for p in range(PASSES)]
-
-        w1_bf = [[sb([P, HALF * PACK], BF16, f"w1_bf{p}_{i}") for i in range(2)] for p in range(PASSES)]
+        w1_bf = [sb([P, H * PACK], BF16, f"w1_bf{p}") for p in range(PASSES)]
+        w1_codes = [sb([P, H], U32, f"w1_codes{p}") for p in range(PASSES)]
+        w1_scales = [sb([P, H], U8, f"w1_scales{p}") for p in range(PASSES)]
 
         def cast_w1(p):
-            for i, engine in enumerate(W1_CAST[p]):
-                cast(
-                    engine,
-                    w1_bf[p][i][:].rearrange("p (t m j) -> p m t j", t=2, j=PACK),
-                    w1_raw[p][:].rearrange("p j (m t) -> p m t j", t=PACK)[:, :, 2 * i : 2 * i + 2, :],
-                )
+            parts = W1_CAST[p]
+            k = PACK // len(parts)
+            dst = w1_bf[p][:].rearrange("p (t m j) -> p m t j", t=PACK, j=PACK)
+            src = w1_raw[p][:].rearrange("p j (m t) -> p m t j", t=PACK)
+            for i, engine in enumerate(parts):
+                cast(engine, dst[:, :, i * k : (i + 1) * k, :], src[:, :, i * k : (i + 1) * k, :])
 
-        def quant_w1(p):
-            for i in range(2):
-                quantize(w1_codes[p][i], w1_scales[p][i], w1_bf[p][i][:])
-
-        w2_bf = [sb([P, HALF * PACK], BF16, f"w2_bf{i}") for i in range(2)]
-        w2_codes = [sb([P, HALF], U32, f"w2_codes{i}") for i in range(2)]
-        w2_scales = [sb([P, HALF], U8, f"w2_scales{i}") for i in range(2)]
+        w2_bf = sb([P, N * PACK], BF16, "w2_bf")
+        w2_codes = sb([P, N], U32, "w2_codes")
+        w2_scales = sb([P, N], U8, "w2_scales")
 
         def cast_w2():
+            k = N // len(W2_CAST)
+            dst = w2_bf[:].rearrange("p (c j) -> p c j", j=PACK)
+            src = w2_raw[:].rearrange("p j c -> p c j")
             for i, engine in enumerate(W2_CAST):
-                cast(
-                    engine,
-                    w2_bf[i][:].rearrange("p (c j) -> p c j", j=PACK),
-                    w2_raw[:].rearrange("p j c -> p c j")[:, i * HALF : (i + 1) * HALF, :],
-                )
+                cast(engine, dst[:, i * k : (i + 1) * k, :], src[:, i * k : (i + 1) * k, :])
 
-        def quant_w2():
-            for i in range(2):
-                quantize(w2_codes[i], w2_scales[i], w2_bf[i][:])
+        x_bf = [sb([P, PASSES, n * PACK], BF16, f"x_bf{c}") for c, n in enumerate(sizes)]
+        x_codes = [sb([P, PASSES, n], U32, f"x_codes{c}") for c, n in enumerate(sizes)]
+        x_scales = [sb([P, PASSES, n], U8, f"x_scales{c}") for c, n in enumerate(sizes)]
 
-        x_bf = [[sb([P, n * PACK], BF16, f"x_bf{c}_{p}") for p in range(PASSES)] for c, (s, n) in enumerate(CHUNKS)]
-        x_codes = [[sb([P, n], U32, f"x_codes{c}_{p}") for p in range(PASSES)] for c, (s, n) in enumerate(CHUNKS)]
-        x_scales = [[sb([P, n], U8, f"x_scales{c}_{p}") for p in range(PASSES)] for c, (s, n) in enumerate(CHUNKS)]
-
-        def cast_x(c, p):
+        def cast_x(c, first_pass, count, engine):
+            g = slice(first_pass, first_pass + count)
             cast(
-                X_CAST[c][p],
-                x_bf[c][p][:].rearrange("p (c j) -> p c j", j=PACK),
-                x_raw[c][p][:].rearrange("p j c -> p c j"),
+                engine,
+                x_bf[c][:, g, :].rearrange("p g (c j) -> p g c j", j=PACK),
+                x_raw[c][:, g].rearrange("p g j c -> p g c j"),
             )
-
-        def quant_x(c, p):
-            quantize(x_codes[c][p], x_scales[c][p], x_bf[c][p][:])
 
         h_ps = {}
 
         def product(c, t, p, bank):
-            cols = slice((t % 2) * P, (t % 2 + 1) * P)
+            cols = slice(t * P, (t + 1) * P)
             nc.tensor.matmul_mx(
                 out=bank,
-                lhsT=w1_codes[p][t // 2][:, cols].bitcast(FP8X4),
-                lhsT_scale=w1_scales[p][t // 2][:, cols],
-                rhs=x_codes[c][p][:].bitcast(FP8X4),
-                rhs_scale=x_scales[c][p][:],
+                lhsT=w1_codes[p][:, cols].bitcast(FP8X4),
+                lhsT_scale=w1_scales[p][:, cols],
+                rhs=x_codes[c][:, p, :].bitcast(FP8X4),
+                rhs_scale=x_scales[c][:, p, :],
                 start=(p == 0),
                 stop=(p == PASSES - 1),
             )
 
-        def first(c, p):
-            n = CHUNKS[c][1]
+        def feed(c, g):
+            n = sizes[c]
+            q = XQ[c]
+            ps = slice(g * q, (g + 1) * q)
+            quantize(
+                x_codes[c][:, ps, :].rearrange("p g n -> p (g n)"),
+                x_scales[c][:, ps, :].rearrange("p g n -> p (g n)"),
+                x_bf[c][:, ps, :].rearrange("p g n -> p (g n)"),
+            )
             if MERGE[c]:
                 return
-            for t in range(PACK):
-                if p == 0:
-                    h_ps[c, t] = psum.tile([P, n], F32, name=f"h_ps{t}", tag=f"h_ps{t}")
-                product(c, t, p, h_ps[c, t][:])
+            for p in range(g * q, (g + 1) * q):
+                for t in range(PACK):
+                    if p == 0:
+                        h_ps[c, t] = psum.tile([P, n], F32, name=f"h_ps{t}", tag=f"h_ps{t}")
+                    product(c, t, p, h_ps[c, t][:])
 
-        relu = [sb([P, PACK, n], F32, f"relu{c}") for c, (s, n) in enumerate(CHUNKS)]
-        h_bf = [sb([P, n * PACK], BF16, f"h_bf{c}") for c, (s, n) in enumerate(CHUNKS)]
-        h_codes = [sb([P, n], U32, f"h_codes{c}") for c, (s, n) in enumerate(CHUNKS)]
-        h_scales = [sb([P, n], U8, f"h_scales{c}") for c, (s, n) in enumerate(CHUNKS)]
-        y_sb = [sb([P, BLOCKS, n], F32, f"y_sb{c}") for c, (s, n) in enumerate(CHUNKS)]
+        relu = [sb([P, PACK, n], F32, f"relu{c}") for c, n in enumerate(sizes)]
+        h_bf = [sb([P, n * PACK], BF16, f"h_bf{c}") for c, n in enumerate(sizes)]
+        h_codes = [sb([P, n], U32, f"h_codes{c}") for c, n in enumerate(sizes)]
+        h_scales = [sb([P, n], U8, f"h_scales{c}") for c, n in enumerate(sizes)]
+        y_sb = [sb([P, BLOCKS, n], F32, f"y_sb{c}") for c, n in enumerate(sizes)]
+
+        def relu_to(engine, out, in_):
+            if engine == "V":
+                nc.vector.tensor_scalar(out, in_, 0.0, None, MAX)
+            else:
+                nc.scalar.activation(out, in_, ACT.Relu)
 
         def hidden(c):
-            n = CHUNKS[c][1]
+            n = sizes[c]
             if MERGE[c]:
                 per = 512 // n
                 for b in range(PACK // per):
-                    bank = psum.tile([P, per, n], F32, name=f"h_ps{b}", tag=f"h_ps{b + 2 * (c % 2)}")
+                    bank = psum.tile([P, per, n], F32, name=f"h_ps{b}", tag=f"h_ps{b + 2 * (c % 2)}" if n < 512 else f"h_ps{b}")
                     for i in range(per):
                         for p in range(PASSES):
                             product(c, b * per + i, p, bank[:, i, :])
@@ -185,73 +185,68 @@ def tile_picked_place_mlp_relu2_sub_l_kernel(tc, xT, w1, w2, gate, offs, out):
                     relu_to(RELU[c][t], relu[c][:, t, :], h_ps[c, t][:])
             src = relu[c][:].rearrange("p t n -> p n t")
             dst = h_bf[c][:].rearrange("p (n t) -> p n t", t=PACK)
-            if SQUARE[c] == "V":
-                nc.vector.tensor_tensor(dst, src, src, MULT)
-            elif SQUARE[c] == "G":
-                nc.gpsimd.tensor_tensor(dst, src, src, MULT)
-            else:
-                nc.scalar.activation(dst, src, ACT.Square)
-            quantize(h_codes[c], h_scales[c], h_bf[c][:])
-
-        def relu_to(engine, out, in_):
-            if engine == "V":
-                nc.vector.tensor_scalar(out, in_, 0.0, None, MAX)
-            else:
-                nc.scalar.activation(out, in_, ACT.Relu)
+            k = n // len(SQUARE[c])
+            for i, engine in enumerate(SQUARE[c]):
+                part = slice(i * k, (i + 1) * k)
+                if engine == "V":
+                    nc.vector.tensor_tensor(dst[:, part, :], src[:, part, :], src[:, part, :], MULT)
+                else:
+                    nc.scalar.activation(dst[:, part, :], src[:, part, :], ACT.Square)
+            quantize(h_codes[c][:], h_scales[c][:], h_bf[c][:])
 
         def second(c):
-            n = CHUNKS[c][1]
+            n = sizes[c]
             per = 512 // n
             for b in range(BLOCKS // per):
                 y_ps = psum.tile([P, per, n], F32, name=f"y_ps{c}_{b}", tag="y_ps", bufs=4)
                 for i in range(per):
                     m = b * per + i
-                    cols = slice((m % 2) * P, (m % 2 + 1) * P)
+                    cols = slice(m * P, (m + 1) * P)
                     nc.tensor.matmul_mx(
                         out=y_ps[:, i, :],
-                        lhsT=w2_codes[m // 2][:, cols].bitcast(FP8X4),
-                        lhsT_scale=w2_scales[m // 2][:, cols],
+                        lhsT=w2_codes[:, cols].bitcast(FP8X4),
+                        lhsT_scale=w2_scales[:, cols],
                         rhs=h_codes[c][:].bitcast(FP8X4),
                         rhs_scale=h_scales[c][:],
                         start=True,
                         stop=True,
                     )
                 blocks = slice(b * per, (b + 1) * per)
-                if not FUSED:
-                    nc.vector.tensor_tensor(y_sb[c][:, blocks, :], y_ps[:], gates[c][:, blocks, :], MULT)
-                elif Y_COPY[c] == "V":
+                if Y_COPY[c] == "V":
                     nc.vector.tensor_copy(out=y_sb[c][:, blocks, :], in_=y_ps[:])
                 else:
                     nc.scalar.copy(out=y_sb[c][:, blocks, :], in_=y_ps[:])
 
         def scatter(c, m):
             s, n = CHUNKS[c]
-            window = windows[m][:].indirect(offsets[:, s // 16 : (s + n) // 16])
-            if FUSED:
-                nc.vector.tensor_tensor(window, y_sb[c][:, m, :], gates[c][:, m, :], MULT)
-            else:
-                nc.vector.tensor_copy(window, y_sb[c][:, m, :])
+            nc.vector.tensor_tensor(
+                windows[m][:].indirect(offsets[:, s // 16 : (s + n) // 16]), y_sb[c][:, m, :], gates[c][:, m, :], MULT
+            )
+
+        def chunk_casts(c):
+            at = 0
+            for segment in X_SEGS[c]:
+                cast_x(c, at, int(segment[1]), segment[0])
+                at += int(segment[1])
+
+        def chunk_feeds(c):
+            for g in range(PASSES // XQ[c]):
+                feed(c, g)
 
         for token in STEPS:
             kind, index = token[0], int(token[1:] or 0)
             if kind == "W":
                 cast_w1(index)
             elif kind == "q":
-                quant_w1(index)
+                quantize(w1_codes[index][:], w1_scales[index][:], w1_bf[index][:])
             elif kind == "c":
-                cast_x(index // 10, index % 10)
+                chunk_casts(index)
             elif kind == "f":
-                quant_x(index // 10, index % 10)
-                first(index // 10, index % 10)
-            elif kind == "X":
-                for p in range(PASSES):
-                    cast_x(index, p)
-                    quant_x(index, p)
-                    first(index, p)
+                chunk_feeds(index)
             elif kind == "V":
                 cast_w2()
             elif kind == "Q":
-                quant_w2()
+                quantize(w2_codes[:], w2_scales[:], w2_bf[:])
             elif kind == "h":
                 hidden(index)
             elif kind == "y":

@@ -99,19 +99,19 @@ def tile_picked_place_mlp_relu2_sub_l_kernel(tc, xT, w1, w2, gate, offs, out):
         def cast_w1(p):
             parts = W1_CAST[p]
             k = PACK // len(parts)
-            dst = w1_bf[p][:].rearrange("p (t m j) -> p m t j", t=PACK, j=PACK)
-            src = w1_raw[p][:].rearrange("p j (m t) -> p m t j", t=PACK)
+            dst = w1_bf[p][:].rearrange("p (t m j) -> p m j t", t=PACK, j=PACK)
+            src = w1_raw[p][:].rearrange("p j (m t) -> p m j t", t=PACK)
             for i, engine in enumerate(parts):
-                cast(engine, dst[:, :, i * k : (i + 1) * k, :], src[:, :, i * k : (i + 1) * k, :])
+                cast(engine, dst[:, :, :, i * k : (i + 1) * k], src[:, :, :, i * k : (i + 1) * k])
 
         w2_bf = sb([P, N * PACK], BF16, "w2_bf")
         w2_codes = sb([P, N], U32, "w2_codes")
         w2_scales = sb([P, N], U8, "w2_scales")
 
         def cast_w2():
-            k = N // len(W2_CAST)
-            dst = w2_bf[:].rearrange("p (c j) -> p c j", j=PACK)
-            src = w2_raw[:].rearrange("p j c -> p c j")
+            k = N // 4 // len(W2_CAST)
+            dst = w2_bf[:].rearrange("p (c i j) -> p c j i", i=4, j=PACK)
+            src = w2_raw[:].rearrange("p j (c i) -> p c j i", i=4)
             for i, engine in enumerate(W2_CAST):
                 cast(engine, dst[:, i * k : (i + 1) * k, :], src[:, i * k : (i + 1) * k, :])
 
@@ -123,8 +123,8 @@ def tile_picked_place_mlp_relu2_sub_l_kernel(tc, xT, w1, w2, gate, offs, out):
             g = slice(first_pass, first_pass + count)
             cast(
                 engine,
-                x_bf[c][:, g, :].rearrange("p g (c j) -> p g c j", j=PACK),
-                x_raw[c][:, g].rearrange("p g j c -> p g c j"),
+                x_bf[c][:, g, :].rearrange("p g (c i j) -> p g c j i", i=4, j=PACK),
+                x_raw[c][:, g].rearrange("p g j (c i) -> p g c j i", i=4),
             )
 
         h_ps = {}
@@ -183,15 +183,15 @@ def tile_picked_place_mlp_relu2_sub_l_kernel(tc, xT, w1, w2, gate, offs, out):
             else:
                 for t in range(PACK):
                     relu_to(RELU[c][t], relu[c][:, t, :], h_ps[c, t][:])
-            src = relu[c][:].rearrange("p t n -> p n t")
-            dst = h_bf[c][:].rearrange("p (n t) -> p n t", t=PACK)
-            k = n // len(SQUARE[c])
+            src = relu[c][:].rearrange("p t (n i) -> p n t i", i=4)
+            dst = h_bf[c][:].rearrange("p (n i t) -> p n t i", i=4, t=PACK)
+            k = n // 4 // len(SQUARE[c])
             for i, engine in enumerate(SQUARE[c]):
                 part = slice(i * k, (i + 1) * k)
                 if engine == "V":
-                    nc.vector.tensor_tensor(dst[:, part, :], src[:, part, :], src[:, part, :], MULT)
+                    nc.vector.tensor_tensor(dst[:, part], src[:, part], src[:, part], MULT)
                 else:
-                    nc.scalar.activation(dst[:, part, :], src[:, part, :], ACT.Square)
+                    nc.scalar.activation(dst[:, part], src[:, part], ACT.Square)
             quantize(h_codes[c][:], h_scales[c][:], h_bf[c][:])
 
         def second(c):

@@ -22,17 +22,18 @@ PASSES = K // (P * PACK)
 BLOCKS = N // P
 
 CHUNKS = [[0,256],[256,256]]
-X_SEGS = [["S1","V2","S1"],["V2","V1","S1"]]
-XQ = [1,2]
-W1_CAST = ["V","SV","S","SV"]
-W2_CAST = "V"
-MERGE = [True,True]
-RELU = ["SSVS","SSVS"]
+X_SEGS = [["S2","V1","V1"],["V1","V1","S1","V1"]]
+XQ = [2,1]
+W1_CAST = ["SV","V","V","VS"]
+W2_CAST = "SV"
+MERGE = [True,False]
+RELU = ["SSSV","SSSS"]
 SQUARE = ["S","S"]
 Y_COPY = ["S","S"]
-LOADS = ["w2","w1","w0","w3","x0","v","x1","o","g0","g1"]
-STEPS = ["V","c0","W3","W1","Q","W0","q3","q0","W2","q2","q1","f0","h0","c1","y0","f1","h1","y1","E01"]
+LOADS = ["w2","w0","w1","x0","w3","v","x1","g0","o","g1"]
+STEPS = ["W0","q0","W3","W2","W1","q2","q3","c0","V","q1","f0","Q","h0","y0","c1","f1","h1","y1","E01"]
 ZERO = "G"
+LATE = []
 
 
 def tile_picked_place_mlp_relu2_sub_l_kernel(tc, xT, w1, w2, gate, offs, out):
@@ -115,15 +116,34 @@ def tile_picked_place_mlp_relu2_sub_l_kernel(tc, xT, w1, w2, gate, offs, out):
             for i, engine in enumerate(W2_CAST):
                 cast(engine, dst[:, i * k : (i + 1) * k, :], src[:, i * k : (i + 1) * k, :])
 
-        x_bf = [sb([P, PASSES, n * PACK], BF16, f"x_bf{c}") for c, n in enumerate(sizes)]
+        def late(c, g):
+            return f"late{LATE.index(g)}" if c == 1 and g in LATE else None
+
+        late_h = [f"late{i}" if i < len(LATE) else None for i in range(2)]
+
+        def tagged(shape, dtype, name, tag):
+            if tag is None:
+                return sb(shape, dtype, name)
+            return held.tile(shape, dtype, name=name, tag=tag, align_bytes=64)
+
+        x_bf = {}
+
+        def x_group(c, g):
+            if (c, g) not in x_bf:
+                x_bf[c, g] = tagged([P, XQ[c], sizes[c] * PACK], BF16, f"x_bf{c}_{g}", late(c, g))
+            return x_bf[c, g]
+
         x_codes = [sb([P, PASSES, n], U32, f"x_codes{c}") for c, n in enumerate(sizes)]
         x_scales = [sb([P, PASSES, n], U8, f"x_scales{c}") for c, n in enumerate(sizes)]
 
         def cast_x(c, first_pass, count, engine):
             g = slice(first_pass, first_pass + count)
+            q = XQ[c]
+            assert first_pass // q == (first_pass + count - 1) // q
+            l = slice(first_pass % q, first_pass % q + count)
             cast(
                 engine,
-                x_bf[c][:, g, :].rearrange("p g (c i j) -> p g c j i", i=4, j=PACK),
+                x_group(c, first_pass // q)[:, l, :].rearrange("p g (c i j) -> p g c j i", i=4, j=PACK),
                 x_raw[c][:, g].rearrange("p g j (c i) -> p g c j i", i=4),
             )
 
@@ -148,7 +168,7 @@ def tile_picked_place_mlp_relu2_sub_l_kernel(tc, xT, w1, w2, gate, offs, out):
             quantize(
                 x_codes[c][:, ps, :].rearrange("p g n -> p (g n)"),
                 x_scales[c][:, ps, :].rearrange("p g n -> p (g n)"),
-                x_bf[c][:, ps, :].rearrange("p g n -> p (g n)"),
+                x_group(c, g)[:].rearrange("p g n -> p (g n)"),
             )
             if MERGE[c]:
                 return
@@ -160,8 +180,8 @@ def tile_picked_place_mlp_relu2_sub_l_kernel(tc, xT, w1, w2, gate, offs, out):
 
         relu = [sb([P, PACK, n], F32, f"relu{c}") for c, n in enumerate(sizes)]
         h_bf = [sb([P, n * PACK], BF16, f"h_bf{c}") for c, n in enumerate(sizes)]
-        h_codes = [sb([P, n], U32, f"h_codes{c}") for c, n in enumerate(sizes)]
-        h_scales = [sb([P, n], U8, f"h_scales{c}") for c, n in enumerate(sizes)]
+        h_codes = [tagged([P, n], U32, f"h_codes{c}", None if c else late_h[0]) for c, n in enumerate(sizes)]
+        h_scales = [tagged([P, n], U8, f"h_scales{c}", None if c else late_h[1]) for c, n in enumerate(sizes)]
         y_sb = [sb([P, BLOCKS, n], F32, f"y_sb{c}") for c, n in enumerate(sizes)]
 
         def relu_to(engine, out, in_):

from contextlib import ExitStack

import concourse.mybir as mybir

K, S, H, N, T = 2048, 512, 512, 512, 1024
FLOPS = 2 * S * (K * H + H * N)

F32 = mybir.dt.float32
BF16 = mybir.dt.bfloat16
U32 = mybir.dt.uint32
U16 = mybir.dt.uint16
U8 = mybir.dt.uint8
FP8X4 = mybir.dt.float8_e4m3fn_x4
ACT = mybir.ActivationFunctionType
MULT = mybir.AluOpType.mult
ADD = mybir.AluOpType.add
MAX = mybir.AluOpType.max

P = 128
PACK = 4
PASSES = K // (P * PACK)
BLOCKS = N // P

CHUNKS = [[0,256],[256,256]]
X_SEGS = [["S2","V1","V1"],["V1","V1","S1","V1"]]
XQ = [2,1]
W1_CAST = ["SV","V","V","VS"]
W2_CAST = "SV"
MERGE = [True,False]
RELU = ["SSSV","SSSS"]
SQUARE = ["S","S"]
Y_COPY = ["S","S"]
LOADS = ["w2","w0","w1","x0","w3","v","x1","g0","o","g1"]
STEPS = ["W0","q0","W3","W2","W1","q2","q3","c0","V","q1","f0","Q","h0","y0","c1","f1","h1","y1","E01"]
ZERO = "G"
LATE = []


def tile_picked_place_mlp_relu2_sub_l_kernel(tc, xT, w1, w2, gate, offs, out):
    nc = tc.nc
    with ExitStack() as ctx:
        held = ctx.enter_context(tc.tile_pool(name="held", bufs=1))
        psum = ctx.enter_context(tc.psum_pool(name="psum", bufs=1))

        def sb(shape, dtype, name):
            return held.tile(shape, dtype, name=name, align_bytes=64)

        offsets = held.tile([P, S // 16], U16, name="offsets")
        warm = sb([P, 16], F32, "warm")
        windows = [sb([P, T], F32, f"window{m}") for m in range(BLOCKS)]
        sizes = [n for s, n in CHUNKS]

        w1_raw = [sb([P, PACK, H], F32, f"w1_raw{p}") for p in range(PASSES)]
        x_raw = [sb([P, PASSES, PACK, n], F32, f"x_raw{c}") for c, n in enumerate(sizes)]
        w2_raw = sb([P, PACK, N], F32, "w2_raw")
        gates = [sb([P, BLOCKS, n], F32, f"gate{c}") for c, n in enumerate(sizes)]

        def rows(p):
            return slice(p * P * PACK, (p + 1) * P * PACK)

        for token in LOADS:
            kind, index = token[0], int(token[1:] or 0)
            if kind == "w":
                nc.sync.dma_start(out=w1_raw[index][:], in_=w1[rows(index), :].rearrange("(p j) w -> p j w", j=PACK))
            elif kind == "x":
                s, n = CHUNKS[index]
                for p in range(PASSES):
                    nc.sync.dma_start(
                        out=x_raw[index][:, p], in_=xT[rows(p), s : s + n].rearrange("(p j) w -> p j w", j=PACK)
                    )
            elif kind == "v":
                nc.sync.dma_start(out=w2_raw[:], in_=w2.rearrange("(p j) w -> p j w", j=PACK))
            elif kind == "o":
                nc.sync.dma_start(offsets[:], offs)
            elif kind == "g":
                s, n = CHUNKS[index]
                nc.sync.dma_start(out=gates[index][:], in_=gate[:, s : s + n].rearrange("(m p) w -> p m w", p=P))

        nc.vector.memset(warm[:], 0.0)
        nc.scalar.activation(warm[:], warm[:], ACT.Relu)
        for m in range(BLOCKS):
            if ZERO == "G":
                nc.gpsimd.memset(windows[m][:], 0.0)
            else:
                nc.vector.memset(windows[m][:], 0.0)

        def cast(engine, out, in_):
            if engine == "V":
                nc.vector.tensor_copy(out=out, in_=in_)
            else:
                nc.scalar.copy(out=out, in_=in_)

        def quantize(codes, scales, grouped):
            nc.vector.quantize_mx(out=codes.bitcast(FP8X4), scales=scales, in_=grouped)

        w1_bf = [sb([P, H * PACK], BF16, f"w1_bf{p}") for p in range(PASSES)]
        w1_codes = [sb([P, H], U32, f"w1_codes{p}") for p in range(PASSES)]
        w1_scales = [sb([P, H], U8, f"w1_scales{p}") for p in range(PASSES)]

        def cast_w1(p):
            parts = W1_CAST[p]
            k = PACK // len(parts)
            dst = w1_bf[p][:].rearrange("p (t m j) -> p m j t", t=PACK, j=PACK)
            src = w1_raw[p][:].rearrange("p j (m t) -> p m j t", t=PACK)
            for i, engine in enumerate(parts):
                cast(engine, dst[:, :, :, i * k : (i + 1) * k], src[:, :, :, i * k : (i + 1) * k])

        w2_bf = sb([P, N * PACK], BF16, "w2_bf")
        w2_codes = sb([P, N], U32, "w2_codes")
        w2_scales = sb([P, N], U8, "w2_scales")

        def cast_w2():
            k = N // 4 // len(W2_CAST)
            dst = w2_bf[:].rearrange("p (c i j) -> p c j i", i=4, j=PACK)
            src = w2_raw[:].rearrange("p j (c i) -> p c j i", i=4)
            for i, engine in enumerate(W2_CAST):
                cast(engine, dst[:, i * k : (i + 1) * k, :], src[:, i * k : (i + 1) * k, :])

        def late(c, g):
            return f"late{LATE.index(g)}" if c == 1 and g in LATE else None

        late_h = [f"late{i}" if i < len(LATE) else None for i in range(2)]

        def tagged(shape, dtype, name, tag):
            if tag is None:
                return sb(shape, dtype, name)
            return held.tile(shape, dtype, name=name, tag=tag, align_bytes=64)

        x_bf = {}

        def x_group(c, g):
            if (c, g) not in x_bf:
                x_bf[c, g] = tagged([P, XQ[c], sizes[c] * PACK], BF16, f"x_bf{c}_{g}", late(c, g))
            return x_bf[c, g]

        x_codes = [sb([P, PASSES, n], U32, f"x_codes{c}") for c, n in enumerate(sizes)]
        x_scales = [sb([P, PASSES, n], U8, f"x_scales{c}") for c, n in enumerate(sizes)]

        def cast_x(c, first_pass, count, engine):
            g = slice(first_pass, first_pass + count)
            q = XQ[c]
            assert first_pass // q == (first_pass + count - 1) // q
            l = slice(first_pass % q, first_pass % q + count)
            cast(
                engine,
                x_group(c, first_pass // q)[:, l, :].rearrange("p g (c i j) -> p g c j i", i=4, j=PACK),
                x_raw[c][:, g].rearrange("p g j (c i) -> p g c j i", i=4),
            )

        h_ps = {}

        def product(c, t, p, bank):
            cols = slice(t * P, (t + 1) * P)
            nc.tensor.matmul_mx(
                out=bank,
                lhsT=w1_codes[p][:, cols].bitcast(FP8X4),
                lhsT_scale=w1_scales[p][:, cols],
                rhs=x_codes[c][:, p, :].bitcast(FP8X4),
                rhs_scale=x_scales[c][:, p, :],
                start=(p == 0),
                stop=(p == PASSES - 1),
            )

        def feed(c, g):
            n = sizes[c]
            q = XQ[c]
            ps = slice(g * q, (g + 1) * q)
            quantize(
                x_codes[c][:, ps, :].rearrange("p g n -> p (g n)"),
                x_scales[c][:, ps, :].rearrange("p g n -> p (g n)"),
                x_group(c, g)[:].rearrange("p g n -> p (g n)"),
            )
            if MERGE[c]:
                return
            for p in range(g * q, (g + 1) * q):
                for t in range(PACK):
                    if p == 0:
                        h_ps[c, t] = psum.tile([P, n], F32, name=f"h_ps{t}", tag=f"h_ps{t}")
                    product(c, t, p, h_ps[c, t][:])

        relu = [sb([P, PACK, n], F32, f"relu{c}") for c, n in enumerate(sizes)]
        h_bf = [sb([P, n * PACK], BF16, f"h_bf{c}") for c, n in enumerate(sizes)]
        h_codes = [tagged([P, n], U32, f"h_codes{c}", None if c else late_h[0]) for c, n in enumerate(sizes)]
        h_scales = [tagged([P, n], U8, f"h_scales{c}", None if c else late_h[1]) for c, n in enumerate(sizes)]
        y_sb = [sb([P, BLOCKS, n], F32, f"y_sb{c}") for c, n in enumerate(sizes)]

        def relu_to(engine, out, in_):
            if engine == "V":
                nc.vector.tensor_scalar(out, in_, 0.0, None, MAX)
            else:
                nc.scalar.activation(out, in_, ACT.Relu)

        def hidden(c):
            n = sizes[c]
            if MERGE[c]:
                per = 512 // n
                for b in range(PACK // per):
                    bank = psum.tile([P, per, n], F32, name=f"h_ps{b}", tag=f"h_ps{b + 2 * (c % 2)}" if n < 512 else f"h_ps{b}")
                    for i in range(per):
                        for p in range(PASSES):
                            product(c, b * per + i, p, bank[:, i, :])
                    relu_to(RELU[c][b], relu[c][:, b * per : (b + 1) * per, :], bank[:])
            else:
                for t in range(PACK):
                    relu_to(RELU[c][t], relu[c][:, t, :], h_ps[c, t][:])
            src = relu[c][:].rearrange("p t (n i) -> p n t i", i=4)
            dst = h_bf[c][:].rearrange("p (n i t) -> p n t i", i=4, t=PACK)
            k = n // 4 // len(SQUARE[c])
            for i, engine in enumerate(SQUARE[c]):
                part = slice(i * k, (i + 1) * k)
                if engine == "V":
                    nc.vector.tensor_tensor(dst[:, part], src[:, part], src[:, part], MULT)
                else:
                    nc.scalar.activation(dst[:, part], src[:, part], ACT.Square)
            quantize(h_codes[c][:], h_scales[c][:], h_bf[c][:])

        def second(c):
            n = sizes[c]
            per = 512 // n
            for b in range(BLOCKS // per):
                y_ps = psum.tile([P, per, n], F32, name=f"y_ps{c}_{b}", tag="y_ps", bufs=4)
                for i in range(per):
                    m = b * per + i
                    cols = slice(m * P, (m + 1) * P)
                    nc.tensor.matmul_mx(
                        out=y_ps[:, i, :],
                        lhsT=w2_codes[:, cols].bitcast(FP8X4),
                        lhsT_scale=w2_scales[:, cols],
                        rhs=h_codes[c][:].bitcast(FP8X4),
                        rhs_scale=h_scales[c][:],
                        start=True,
                        stop=True,
                    )
                blocks = slice(b * per, (b + 1) * per)
                if Y_COPY[c] == "V":
                    nc.vector.tensor_copy(out=y_sb[c][:, blocks, :], in_=y_ps[:])
                else:
                    nc.scalar.copy(out=y_sb[c][:, blocks, :], in_=y_ps[:])

        def scatter(c, m):
            s, n = CHUNKS[c]
            nc.vector.tensor_tensor(
                windows[m][:].indirect(offsets[:, s // 16 : (s + n) // 16]), y_sb[c][:, m, :], gates[c][:, m, :], MULT
            )

        def chunk_casts(c):
            at = 0
            for segment in X_SEGS[c]:
                cast_x(c, at, int(segment[1]), segment[0])
                at += int(segment[1])

        def chunk_feeds(c):
            for g in range(PASSES // XQ[c]):
                feed(c, g)

        for token in STEPS:
            kind, index = token[0], int(token[1:] or 0)
            if kind == "W":
                cast_w1(index)
            elif kind == "q":
                quantize(w1_codes[index][:], w1_scales[index][:], w1_bf[index][:])
            elif kind == "c":
                chunk_casts(index)
            elif kind == "f":
                chunk_feeds(index)
            elif kind == "V":
                cast_w2()
            elif kind == "Q":
                quantize(w2_codes[:], w2_scales[:], w2_bf[:])
            elif kind == "h":
                hidden(index)
            elif kind == "y":
                second(index)
            elif kind == "S":
                for m in range(BLOCKS):
                    scatter(index, m)
            elif kind == "E":
                for m in range(BLOCKS):
                    for c in token[1:]:
                        scatter(int(c), m)
                    nc.sync.dma_start(out=out[m * P : (m + 1) * P, :], in_=windows[m][:])
